import numpy as np
CORES = [4,20,60,84,92,100,116]
N = 7
F = 64
def setup_inputs(rng):
    m = (rng.standard_normal((N, 128, 128), dtype=np.float32) / 11)
    return {"m": m, "mt": m.transpose(0, 2, 1).copy(), "x": rng.standard_normal((N, 128, F), dtype=np.float32)}
def setup_inputs_big(rng):
    d = setup_inputs(rng)
    for k in ("x",): d[k] = (d[k].astype(np.float32) * 1048576.0).astype(d[k].dtype)
    return d
def setup_inputs_small(rng):
    d = setup_inputs(rng)
    for k in ("x",): d[k] = (d[k].astype(np.float32) * (1 / 1048576.0)).astype(d[k].dtype)
    return d
def setup_inputs_apart(rng):
    d = setup_inputs(rng)
    f = (10.0 ** rng.permutation(np.linspace(-1.5, 1.5, N))).astype(np.float32).reshape(N, 1, 1)
    for k in ("x",): d[k] = (d[k].astype(np.float32) * f).astype(d[k].dtype)
    return d
def reference(m, mt, x):
    M, X = m.astype(np.float64), x.astype(np.float64)
    y = np.zeros((N, 128, F)); p = X[0]
    for r in range(N):
        p = M[r].T @ p
        y[r] = p
    return {"y": y.astype(np.float32)}

@@ -1,0 +1,176 @@
+from concourse.bass import DstId, RemoteDMATransfer
+
+K_P_ON = 8
+K_STAGE = 8
+K_OFF = 8
+
+_S64 = ["bx"] + ["p%d" % i for i in range(7)]
+_S128 = ["bm", "m1", "m2", "m3", "m4", "m5", "R1", "R2"]
+_DRAM = ["dm", "dmt", "dl"]
+_OUTS = ["p%d" % i for i in range(7)] + ["R1", "R2"]
+_WIDTH = {}
+SCRATCH = {}
+for _b in _S64:
+    SCRATCH[_b] = ("sbuf", [128, 64], "float32")
+    _WIDTH[_b] = 64
+for _b in _S128:
+    SCRATCH[_b] = ("sbuf", [128, 128], "float32")
+    _WIDTH[_b] = 128
+for _b in _DRAM:
+    SCRATCH[_b] = ("dram", [128, 128], "float32")
+    _WIDTH[_b] = 128
+for _i in range(7):
+    SCRATCH["ps%d" % _i] = ("psum", [128, 512], "float32")
+
+SEMAPHORES = ["sent", "st"] + ["r_" + b for b in _S64 + _S128 + _DRAM] + ["mm_" + b for b in _OUTS]
+
+
+def _plan(T, topo):
+    R = list(T.cores)
+    ncores = topo.CHIPS * topo.CORES_PER_CHIP
+    plan = {}
+
+    def P(c):
+        return plan.setdefault(c, {"loads": [], "calls": [], "stages": [], "store": None})
+
+    def owners(src, dst):
+        own = [c for c in range(ncores) if topo.chip(c) == topo.chip(src) and T.rank_of(c) is None
+               and topo.may_write(c, dst)]
+        return ([c for c in own if topo.die(c) == topo.die(src)], [c for c in own if topo.die(c) != topo.die(src)])
+
+    def relay(h, land, dst):
+        P(h)["calls"].append([("dl", land, [dst], K_OFF)])
+
+    same0, _ = owners(R[0], R[2])
+    ha, hb = same0[0], same0[1]
+
+    p = P(R[0])
+    p["loads"] = [("sync", "bx", "x"), ("scalar", "bm", "m")]
+    p["stages"] = [("p0", "bm", "bx")]
+    p["calls"] = [[("p0", "p0", [ha, hb], K_P_ON)], [("p0", "p0", [R[6], R[5], R[3], R[1]], K_OFF)]]
+    p["store"] = "p0"
+
+    p = P(R[1])
+    p["loads"] = [("sync", "dm", "m"), ("sync", "bm", "m")]
+    p["calls"] = [[("dm", "dl", [hb], K_STAGE)], [("dm", "m1", [ha], K_OFF)],
+                  [("dm", "m1", [R[6], R[5], R[3]], K_OFF)]]
+    p["stages"] = [("p1", "bm", "p0")]
+    p["store"] = "p1"
+
+    p = P(ha)
+    p["stages"] = [("p1", "m1", "p0")]
+    p["calls"] = [[("dl", "m3", [R[4]], K_OFF)], [("p1", "p1", [R[4]], K_OFF)]]
+    P(hb)["calls"] = [[("dl", "m1", [R[2]], K_OFF)], [("p0", "p0", [R[2]], K_OFF)]]
+
+    s, o = owners(R[2], R[3])
+    p = P(R[2])
+    p["loads"] = [("sync", "dm", "m"), ("sync", "dmt", "mt"), ("sync", "bm", "m")]
+    p["calls"] = [[("dm", "dl", [s[0], o[0], s[1]], K_STAGE)], [("dmt", "m2", [R[4]], K_OFF)]]
+    p["stages"] = [("p1", "m1", "p0"), ("p2", "bm", "p1")]
+    p["store"] = "p2"
+    relay(s[0], "m2", R[6])
+    relay(o[0], "m2", R[5])
+    relay(s[1], "m2", R[3])
+
+    p = P(R[3])
+    p["loads"] = [("sync", "dmt", "mt"), ("sync", "dm", "m"), ("sync", "bm", "m")]
+    p["calls"] = [[("dmt", "dl", [ha], K_STAGE)], [("dm", "m3", [R[6], R[5]], K_OFF)]]
+    p["stages"] = [("p1", "m1", "p0"), ("p2", "m2", "p1"), ("p3", "bm", "p2")]
+    p["store"] = "p3"
+
+    s, o = owners(R[4], R[5])
+    p = P(R[4])
+    p["loads"] = [("sync", "dm", "m"), ("sync", "bm", "m")]
+    p["calls"] = [[("dm", "dl", [o[0], s[0]], K_STAGE)]]
+    p["stages"] = [("R1", "m3", "bm"), ("R2", "m2", "R1"), ("p4", "R2", "p1")]
+    p["store"] = "p4"
+    relay(o[0], "m4", R[6])
+    relay(s[0], "m4", R[5])
+
+    p = P(R[5])
+    p["loads"] = [("sync", "dmt", "mt"), ("sync", "bm", "m")]
+    p["calls"] = [[("dmt", "m5", [R[6]], K_OFF)]]
+    p["stages"] = [("p1", "m1", "p0"), ("p2", "m2", "p1"), ("p3", "m3", "p2"), ("p4", "m4", "p3"), ("p5", "bm", "p4")]
+    p["store"] = "p5"
+
+    p = P(R[6])
+    p["loads"] = [("sync", "bm", "m")]
+    p["stages"] = [("R1", "m5", "bm"), ("p1", "m1", "p0"), ("p2", "m2", "p1"), ("p3", "m3", "p2"), ("p4", "m4", "p3"),
+                   ("p6", "R1", "p4")]
+    p["store"] = "p6"
+    return plan
+
+
+def _low_bits(mask, k):
+    out, b = 0, 1
+    while k > 0:
+        if mask & b:
+            out |= b
+            k -= 1
+        b <<= 1
+    return out
+
+
+def rank_program(g, core, T, topo):
+    plan = _plan(T, topo)
+    me = plan.get(core)
+    if me is None:
+        return
+
+    ready = {}
+    for _q, buf, _src in me["loads"]:
+        ready[buf] = 16
+    for out, _l, _r in me["stages"]:
+        ready[out] = 1
+    for src_core in plan:
+        for call in plan[src_core]["calls"]:
+            for _s, land, dsts, k in call:
+                if core in dsts:
+                    ready[land] = k
+
+    def wait(queue, buf):
+        queue.wait_ge(T.sem["r_" + buf], ready[buf])
+
+    for q, buf, src in me["loads"]:
+        queue = g.sync if q == "sync" else g.scalar
+        queue.dma_start(T[buf][:], T[src][:]).then_inc(T.sem["r_" + buf], 16)
+
+    for i, (out, lhsT, rhs) in enumerate(me["stages"]):
+        n = _WIDTH[out]
+        ps = T["ps%d" % i]
+        wait(g.tensor, lhsT)
+        wait(g.tensor, rhs)
+        g.tensor.matmul(ps[:, 0:n], T[lhsT][:], T[rhs][:], start=True, stop=True).then_inc(T.sem["mm_" + out], 1)
+        g.vector.wait_ge(T.sem["mm_" + out], 1)
+        g.vector.tensor_copy(T[out][:], ps[:, 0:n]).then_inc(T.sem["r_" + out], 1)
+
+    if me["store"] is not None:
+        wait(g.sync, me["store"])
+        g.sync.dma_start(T.y[:], T[me["store"]][:]).then_inc(T.sem.st, 16)
+        g.sync.wait_ge(T.sem.st, 16)
+
+    sent = 0
+    for call in me["calls"]:
+        transfers = []
+        for src, land, dsts, k in call:
+            wait(g, src)
+            mask = topo.mask(core, dsts[0])
+            for d in dsts:
+                assert topo.may_write(core, d)
+                mask &= topo.mask(core, d)
+            mask = _low_bits(mask, k)
+            sent += k
+            transfers.append((src, land, dsts, mask))
+        if len(transfers) == 1 and len(transfers[0][2]) == 1:
+            src, land, dsts, mask = transfers[0]
+            rid, pid, _se = topo.addr(dsts[0])
+            g.remote_dma(T[land][:], T[src][:], T.sem["r_" + land], T.sem.sent, pid, rid, mask)
+        else:
+            g.remote_dma_fused(
+                [RemoteDMATransfer(dst_ids=[DstId(rid=topo.addr(d)[0], pnc=topo.addr(d)[1]) for d in dsts],
+                                   dma_engine_mask=mask, remote_sem=T.sem["r_" + land],
+                                   srcs=[T[src][:]], dsts=[T[land][:] for _d in dsts], alu_op=0)
+                 for src, land, dsts, mask in transfers],
+                local_sem=T.sem.sent)
+    if sent:
+        g.wait_ge(T.sem.sent, sent)

@@ -1,6 +1,5 @@
 from concourse.bass import DstId, RemoteDMATransfer
 
-K_P_ON = 8
 K_STAGE = 8
 K_OFF = 8
 
@@ -38,34 +37,39 @@ def _plan(T, topo):
                and topo.may_write(c, dst)]
         return ([c for c in own if topo.die(c) == topo.die(src)], [c for c in own if topo.die(c) != topo.die(src)])
 
-    def relay(h, land, dst):
-        P(h)["calls"].append([("dl", land, [dst], K_OFF)])
+    def width(src, dst):
+        return bin(topo.mask(src, dst)).count("1")
 
-    same0, _ = owners(R[0], R[2])
-    ha, hb = same0[0], same0[1]
+    def relay(h, land, dst):
+        P(h)["calls"].append([("dl", land, [dst], K_OFF, 0)])
+
+    same1, _ = owners(R[1], R[2])
+    ha, hb = same1[0], same1[1]
 
     p = P(R[0])
     p["loads"] = [("sync", "bx", "x"), ("scalar", "bm", "m")]
     p["stages"] = [("p0", "bm", "bx")]
-    p["calls"] = [[("p0", "p0", [ha, hb], K_P_ON)], [("p0", "p0", [R[6], R[5], R[3], R[1]], K_OFF)]]
+    p["calls"] = [[("p0", "p0", [ha, hb], K_OFF, 0)], [("p0", "p0", [R[6], R[5], R[3], R[1]], K_OFF, 0)]]
     p["store"] = "p0"
 
+    off = width(R[1], R[6])
+    rest = (width(R[1], ha) - off) // 2
     p = P(R[1])
     p["loads"] = [("sync", "dm", "m"), ("sync", "bm", "m")]
-    p["calls"] = [[("dm", "dl", [hb], K_STAGE)], [("dm", "m1", [ha], K_OFF)],
-                  [("dm", "m1", [R[6], R[5], R[3]], K_OFF)]]
+    p["calls"] = [[("dm", "m1", [R[6], R[5], R[3]], off, 0), ("dm", "m1", [ha], rest, off),
+                   ("dm", "dl", [hb], rest, off + rest)]]
     p["stages"] = [("p1", "bm", "p0")]
     p["store"] = "p1"
 
     p = P(ha)
     p["stages"] = [("p1", "m1", "p0")]
-    p["calls"] = [[("dl", "m3", [R[4]], K_OFF)], [("p1", "p1", [R[4]], K_OFF)]]
-    P(hb)["calls"] = [[("dl", "m1", [R[2]], K_OFF)], [("p0", "p0", [R[2]], K_OFF)]]
+    p["calls"] = [[("dl", "m3", [R[4]], K_OFF, 0)], [("p1", "p1", [R[4]], K_OFF, 0)]]
+    P(hb)["calls"] = [[("dl", "m1", [R[2]], K_OFF, 0)], [("p0", "p0", [R[2]], K_OFF, 0)]]
 
     s, o = owners(R[2], R[3])
     p = P(R[2])
-    p["loads"] = [("sync", "dm", "m"), ("sync", "dmt", "mt"), ("sync", "bm", "m")]
-    p["calls"] = [[("dm", "dl", [s[0], o[0], s[1]], K_STAGE)], [("dmt", "m2", [R[4]], K_OFF)]]
+    p["loads"] = [("sync", "dm", "m"), ("sync", "bm", "m")]
+    p["calls"] = [[("dm", "dl", [s[0], o[0], s[1]], K_STAGE, 0)], [("dm", "m2", [R[4]], K_OFF, 0)]]
     p["stages"] = [("p1", "m1", "p0"), ("p2", "bm", "p1")]
     p["store"] = "p2"
     relay(s[0], "m2", R[6])
@@ -74,39 +78,46 @@ def _plan(T, topo):
 
     p = P(R[3])
     p["loads"] = [("sync", "dmt", "mt"), ("sync", "dm", "m"), ("sync", "bm", "m")]
-    p["calls"] = [[("dmt", "dl", [ha], K_STAGE)], [("dm", "m3", [R[6], R[5]], K_OFF)]]
+    p["calls"] = [[("dmt", "dl", [ha], K_STAGE, 0)], [("dm", "m3", [R[6], R[5]], K_OFF, 0)]]
     p["stages"] = [("p1", "m1", "p0"), ("p2", "m2", "p1"), ("p3", "bm", "p2")]
     p["store"] = "p3"
 
     s, o = owners(R[4], R[5])
     p = P(R[4])
-    p["loads"] = [("sync", "dm", "m"), ("sync", "bm", "m")]
-    p["calls"] = [[("dm", "dl", [o[0], s[0]], K_STAGE)]]
-    p["stages"] = [("R1", "m3", "bm"), ("R2", "m2", "R1"), ("p4", "R2", "p1")]
+    p["loads"] = [("sync", "dmt", "mt"), ("sync", "bm", "m")]
+    p["calls"] = [[("dmt", "dl", [o[0], s[0]], K_STAGE, 0)]]
+    p["stages"] = [("R1", "m3", "bm"), ("p2", "m2", "p1"), ("p4", "R1", "p2")]
     p["store"] = "p4"
     relay(o[0], "m4", R[6])
     relay(s[0], "m4", R[5])
 
     p = P(R[5])
     p["loads"] = [("sync", "dmt", "mt"), ("sync", "bm", "m")]
-    p["calls"] = [[("dmt", "m5", [R[6]], K_OFF)]]
-    p["stages"] = [("p1", "m1", "p0"), ("p2", "m2", "p1"), ("p3", "m3", "p2"), ("p4", "m4", "p3"), ("p5", "bm", "p4")]
+    p["calls"] = [[("dmt", "m5", [R[6]], K_OFF, 0)]]
+    p["stages"] = [("p1", "m1", "p0"), ("p2", "m2", "p1"), ("R1", "m4", "bm"), ("p3", "m3", "p2"), ("p5", "R1", "p3")]
     p["store"] = "p5"
 
     p = P(R[6])
     p["loads"] = [("sync", "bm", "m")]
-    p["stages"] = [("R1", "m5", "bm"), ("p1", "m1", "p0"), ("p2", "m2", "p1"), ("p3", "m3", "p2"), ("p4", "m4", "p3"),
-                   ("p6", "R1", "p4")]
+    p["stages"] = [("R1", "m5", "bm"), ("p1", "m1", "p0"), ("p2", "m2", "p1"), ("R2", "m4", "R1"), ("p3", "m3", "p2"),
+                   ("p6", "R2", "p3")]
     p["store"] = "p6"
+
+    for c in plan:
+        plan[c]["calls"] = [[(src, land, dsts, min([k] + [width(c, d) - skip for d in dsts]), skip)
+                             for src, land, dsts, k, skip in call] for call in plan[c]["calls"]]
     return plan
 
 
-def _low_bits(mask, k):
+def _bits(mask, k, skip):
     out, b = 0, 1
     while k > 0:
         if mask & b:
-            out |= b
-            k -= 1
+            if skip > 0:
+                skip -= 1
+            else:
+                out |= b
+                k -= 1
         b <<= 1
     return out
 
@@ -124,7 +135,7 @@ def rank_program(g, core, T, topo):
         ready[out] = 1
     for src_core in plan:
         for call in plan[src_core]["calls"]:
-            for _s, land, dsts, k in call:
+            for _s, land, dsts, k, _skip in call:
                 if core in dsts:
                     ready[land] = k
 
@@ -152,15 +163,14 @@ def rank_program(g, core, T, topo):
     sent = 0
     for call in me["calls"]:
         transfers = []
-        for src, land, dsts, k in call:
+        for src, land, dsts, k, skip in call:
             wait(g, src)
             mask = topo.mask(core, dsts[0])
             for d in dsts:
                 assert topo.may_write(core, d)
                 mask &= topo.mask(core, d)
-            mask = _low_bits(mask, k)
             sent += k
-            transfers.append((src, land, dsts, mask))
+            transfers.append((src, land, dsts, _bits(mask, k, skip)))
         if len(transfers) == 1 and len(transfers[0][2]) == 1:
             src, land, dsts, mask = transfers[0]
             rid, pid, _se = topo.addr(dsts[0])

from concourse.bass import DstId, RemoteDMATransfer

K_STAGE = 8
K_OFF = 8

_S64 = ["bx"] + ["p%d" % i for i in range(7)]
_S128 = ["bm", "m1", "m2", "m3", "m4", "m5", "R1", "R2"]
_DRAM = ["dm", "dmt", "dl"]
_OUTS = ["p%d" % i for i in range(7)] + ["R1", "R2"]
_WIDTH = {}
SCRATCH = {}
for _b in _S64:
    SCRATCH[_b] = ("sbuf", [128, 64], "float32")
    _WIDTH[_b] = 64
for _b in _S128:
    SCRATCH[_b] = ("sbuf", [128, 128], "float32")
    _WIDTH[_b] = 128
for _b in _DRAM:
    SCRATCH[_b] = ("dram", [128, 128], "float32")
    _WIDTH[_b] = 128
for _i in range(7):
    SCRATCH["ps%d" % _i] = ("psum", [128, 512], "float32")

SEMAPHORES = ["sent", "st"] + ["r_" + b for b in _S64 + _S128 + _DRAM] + ["mm_" + b for b in _OUTS]


def _plan(T, topo):
    R = list(T.cores)
    ncores = topo.CHIPS * topo.CORES_PER_CHIP
    plan = {}

    def P(c):
        return plan.setdefault(c, {"loads": [], "calls": [], "stages": [], "store": None})

    def owners(src, dst):
        own = [c for c in range(ncores) if topo.chip(c) == topo.chip(src) and T.rank_of(c) is None
               and topo.may_write(c, dst)]
        return ([c for c in own if topo.die(c) == topo.die(src)], [c for c in own if topo.die(c) != topo.die(src)])

    def width(src, dst):
        return bin(topo.mask(src, dst)).count("1")

    def relay(h, land, dst):
        P(h)["calls"].append([("dl", land, [dst], K_OFF, 0)])

    same1, _ = owners(R[1], R[2])
    ha, hb = same1[0], same1[1]

    p = P(R[0])
    p["loads"] = [("sync", "bx", "x"), ("scalar", "bm", "m")]
    p["stages"] = [("p0", "bm", "bx")]
    p["calls"] = [[("p0", "p0", [ha, hb], K_OFF, 0)], [("p0", "p0", [R[6], R[5], R[3], R[1]], K_OFF, 0)]]
    p["store"] = "p0"

    off = width(R[1], R[6])
    rest = (width(R[1], ha) - off) // 2
    p = P(R[1])
    p["loads"] = [("sync", "dm", "m"), ("sync", "bm", "m")]
    p["calls"] = [[("dm", "m1", [R[6], R[5], R[3]], off, 0), ("dm", "m1", [ha], rest, off),
                   ("dm", "dl", [hb], rest, off + rest)]]
    p["stages"] = [("p1", "bm", "p0")]
    p["store"] = "p1"

    p = P(ha)
    p["stages"] = [("p1", "m1", "p0")]
    p["calls"] = [[("dl", "m3", [R[4]], K_OFF, 0)], [("p1", "p1", [R[4]], K_OFF, 0)]]
    P(hb)["calls"] = [[("dl", "m1", [R[2]], K_OFF, 0)], [("p0", "p0", [R[2]], K_OFF, 0)]]

    s, o = owners(R[2], R[3])
    p = P(R[2])
    p["loads"] = [("sync", "dm", "m"), ("sync", "bm", "m")]
    p["calls"] = [[("dm", "dl", [s[0], o[0], s[1]], K_STAGE, 0)], [("dm", "m2", [R[4]], K_OFF, 0)]]
    p["stages"] = [("p1", "m1", "p0"), ("p2", "bm", "p1")]
    p["store"] = "p2"
    relay(s[0], "m2", R[6])
    relay(o[0], "m2", R[5])
    relay(s[1], "m2", R[3])

    p = P(R[3])
    p["loads"] = [("sync", "dmt", "mt"), ("sync", "dm", "m"), ("sync", "bm", "m")]
    p["calls"] = [[("dmt", "dl", [ha], K_STAGE, 0)], [("dm", "m3", [R[6], R[5]], K_OFF, 0)]]
    p["stages"] = [("p1", "m1", "p0"), ("p2", "m2", "p1"), ("p3", "bm", "p2")]
    p["store"] = "p3"

    s, o = owners(R[4], R[5])
    p = P(R[4])
    p["loads"] = [("sync", "dmt", "mt"), ("sync", "bm", "m")]
    p["calls"] = [[("dmt", "dl", [o[0], s[0]], K_STAGE, 0)]]
    p["stages"] = [("R1", "m3", "bm"), ("p2", "m2", "p1"), ("p4", "R1", "p2")]
    p["store"] = "p4"
    relay(o[0], "m4", R[6])
    relay(s[0], "m4", R[5])

    p = P(R[5])
    p["loads"] = [("sync", "dmt", "mt"), ("sync", "bm", "m")]
    p["calls"] = [[("dmt", "m5", [R[6]], K_OFF, 0)]]
    p["stages"] = [("p1", "m1", "p0"), ("p2", "m2", "p1"), ("R1", "m4", "bm"), ("p3", "m3", "p2"), ("p5", "R1", "p3")]
    p["store"] = "p5"

    p = P(R[6])
    p["loads"] = [("sync", "bm", "m")]
    p["stages"] = [("R1", "m5", "bm"), ("p1", "m1", "p0"), ("p2", "m2", "p1"), ("R2", "m4", "R1"), ("p3", "m3", "p2"),
                   ("p6", "R2", "p3")]
    p["store"] = "p6"

    for c in plan:
        plan[c]["calls"] = [[(src, land, dsts, min([k] + [width(c, d) - skip for d in dsts]), skip)
                             for src, land, dsts, k, skip in call] for call in plan[c]["calls"]]
    return plan


def _bits(mask, k, skip):
    out, b = 0, 1
    while k > 0:
        if mask & b:
            if skip > 0:
                skip -= 1
            else:
                out |= b
                k -= 1
        b <<= 1
    return out


def rank_program(g, core, T, topo):
    plan = _plan(T, topo)
    me = plan.get(core)
    if me is None:
        return

    ready = {}
    for _q, buf, _src in me["loads"]:
        ready[buf] = 16
    for out, _l, _r in me["stages"]:
        ready[out] = 1
    for src_core in plan:
        for call in plan[src_core]["calls"]:
            for _s, land, dsts, k, _skip in call:
                if core in dsts:
                    ready[land] = k

    def wait(queue, buf):
        queue.wait_ge(T.sem["r_" + buf], ready[buf])

    for q, buf, src in me["loads"]:
        queue = g.sync if q == "sync" else g.scalar
        queue.dma_start(T[buf][:], T[src][:]).then_inc(T.sem["r_" + buf], 16)

    for i, (out, lhsT, rhs) in enumerate(me["stages"]):
        n = _WIDTH[out]
        ps = T["ps%d" % i]
        wait(g.tensor, lhsT)
        wait(g.tensor, rhs)
        g.tensor.matmul(ps[:, 0:n], T[lhsT][:], T[rhs][:], start=True, stop=True).then_inc(T.sem["mm_" + out], 1)
        g.vector.wait_ge(T.sem["mm_" + out], 1)
        g.vector.tensor_copy(T[out][:], ps[:, 0:n]).then_inc(T.sem["r_" + out], 1)

    if me["store"] is not None:
        wait(g.sync, me["store"])
        g.sync.dma_start(T.y[:], T[me["store"]][:]).then_inc(T.sem.st, 16)
        g.sync.wait_ge(T.sem.st, 16)

    sent = 0
    for call in me["calls"]:
        transfers = []
        for src, land, dsts, k, skip in call:
            wait(g, src)
            mask = topo.mask(core, dsts[0])
            for d in dsts:
                assert topo.may_write(core, d)
                mask &= topo.mask(core, d)
            sent += k
            transfers.append((src, land, dsts, _bits(mask, k, skip)))
        if len(transfers) == 1 and len(transfers[0][2]) == 1:
            src, land, dsts, mask = transfers[0]
            rid, pid, _se = topo.addr(dsts[0])
            g.remote_dma(T[land][:], T[src][:], T.sem["r_" + land], T.sem.sent, pid, rid, mask)
        else:
            g.remote_dma_fused(
                [RemoteDMATransfer(dst_ids=[DstId(rid=topo.addr(d)[0], pnc=topo.addr(d)[1]) for d in dsts],
                                   dma_engine_mask=mask, remote_sem=T.sem["r_" + land],
                                   srcs=[T[src][:]], dsts=[T[land][:] for _d in dsts], alu_op=0)
                 for src, land, dsts, mask in transfers],
                local_sem=T.sem.sent)
    if sent:
        g.wait_ge(T.sem.sent, sent)
